import numpy as np
import ml_dtypes


def mxq(x, axis, fmt="e4m3"):
    dtype, down = {"e4m3": (ml_dtypes.float8_e4m3fn, 7), "e5m2": (ml_dtypes.float8_e5m2, 14)}[fmt]
    v = np.moveaxis(np.asarray(x, np.float32).astype(ml_dtypes.bfloat16).astype(np.float64), axis, -1)
    blocks = v.reshape(v.shape[:-1] + (-1, 32))
    amax = np.abs(blocks).max(-1, keepdims=True)
    byte = np.maximum(np.where(amax > 0, np.frexp(amax)[1] - 1 + 127, 0) - down, 1)
    scale = np.exp2(byte - 127.0)
    codes = (blocks / scale).astype(np.float32).astype(dtype).astype(np.float64)
    return np.moveaxis((codes * scale).reshape(v.shape), -1, axis)


WIDE = False


def mx_kscale(k):
    if not WIDE:
        return np.ones(k)
    levels = np.array([10, -10, 5, -5, 0])
    if k % 512:
        return np.exp2(np.random.permutation(np.resize(levels, k // 32))).repeat(32)
    a = np.empty((k // 512, 16))
    for p in range(k // 512):
        a[p, :8] = np.random.permutation(np.resize(levels, 8))
        for g in range(8):
            far = levels[np.abs(levels - a[p, g]) >= 10]
            a[p, g + 8] = far[np.random.randint(len(far))]
    return np.exp2(a.ravel()).repeat(32)


def f64(x):
    return np.asarray(x).astype(np.float64)


def striped(idx):
    return np.tile(idx.reshape(-1, 16).T, (8, 1)).astype(np.uint16)


def unstriped(offs):
    return offs[:16].T.reshape(-1).astype(np.int64)


E2M1 = np.array([0.0, 0.5, 1.0, 1.5, 2.0, 3.0, 4.0, 6.0, -0.0, -0.5, -1.0, -1.5, -2.0, -3.0, -4.0, -6.0])


def pack_weight(w, fmt):
    k, n = w.shape
    w = f64(np.asarray(w, np.float32).astype(ml_dtypes.bfloat16)).reshape(k // 32, 32, n)
    amax = np.abs(w).max(1)
    if fmt == "e4m3":
        byte = np.frexp(amax)[1] - 1 + 127 - 7
    else:
        mant, ex = np.frexp(amax / 6.0)
        byte = np.where(mant > 0.5, ex, ex - 1) + 127
    byte = np.clip(np.where(amax > 0, byte, 1), 1, 254)
    scaled = (w * np.exp2(127.0 - byte)[:, None, :]).reshape(k, n).astype(np.float32)
    by_word = np.ascontiguousarray(scaled.reshape(k // 512, 128, 4, n).transpose(0, 1, 3, 2))
    if fmt == "e4m3":
        words = by_word.astype(ml_dtypes.float8_e4m3fn).view(np.uint8)
    else:
        c = by_word.astype(ml_dtypes.float4_e2m1fn).view(np.uint8) & 0xF
        words = (c[..., 0::2] | (c[..., 1::2] << 4)).reshape(k // 512, 128, 2 * n)
    return np.ascontiguousarray(words), np.ascontiguousarray(byte.astype(np.uint8).reshape(k // 512, 16, n))


def unpack_weight(words, scales, fmt):
    g, _, n = scales.shape
    words = np.ascontiguousarray(words).reshape(g, 128, n, -1)
    if fmt == "e4m3":
        vals = words.view(ml_dtypes.float8_e4m3fn).astype(np.float64)
    else:
        nib = np.empty((g, 128, n, 4), np.uint8)
        nib[..., 0::2] = words & 0xF
        nib[..., 1::2] = words >> 4
        vals = E2M1[nib]
    vals = vals * np.repeat(np.exp2(scales.astype(np.float64) - 127.0), 8, axis=1)[..., None]
    return vals.transpose(0, 1, 3, 2).reshape(g * 512, n)


def gelu(v):
    return 0.5 * v * (1.0 + np.tanh(np.sqrt(2.0 / np.pi) * (v + 0.044715 * v**3)))


T, S, K, H, N = 2048, 1024, 1024, 1024, 768

def setup_inputs():
    n = np.random.standard_normal
    s = mx_kscale(K)[:, None]
    u = mx_kscale(H)[:, None]
    v = n((K, T)) * s
    w1 = n((K, H)) / np.sqrt(K) / s * u.T
    w4 = n((H, N)) * np.sqrt(2.0 / H) / u
    wd = n((K, N)) / np.sqrt(K) / s
    tab_words, tab_scales = pack_weight(v, "e4m3")
    w4_words, w4_scales = pack_weight(w4, "e2m1")
    wd_words, wd_scales = pack_weight(wd, "e4m3")
    return {
        "tab_words": tab_words, "tab_scales": tab_scales,
        "offs": striped(np.random.permutation(T)[:S]),
        "gT": np.exp(0.3 * n((N, T))).astype(np.float32),
        "w1": w1.astype(np.float32),
        "w4_words": w4_words, "w4_scales": w4_scales,
        "wd_words": wd_words, "wd_scales": wd_scales,
    }

def reference(tab_words, tab_scales, offs, gT, w1, w4_words, w4_scales, wd_words, wd_scales):
    v = unpack_weight(tab_words, tab_scales, "e4m3")[:, unstriped(offs)]
    g = f64(gT)[:, unstriped(offs)]
    w1q = mxq(f64(w1), 0, "e4m3")
    w4 = unpack_weight(w4_words, w4_scales, "e2m1")
    wd = unpack_weight(wd_words, wd_scales, "e4m3")
    h = np.maximum(w1q.T @ v, 0.0)
    hq = mxq(h, 0, "e4m3")
    y = w4.T @ hq + wd.T @ v
    return np.log(1.0 + np.maximum(y, 0.0)) * g

@@ -1,0 +1,209 @@
+from contextlib import ExitStack
+
+import concourse.mybir as mybir
+
+T, S, K, H, N = 2048, 1024, 1024, 1024, 768
+FLOPS = 2 * S * (K * H + H * N + K * N)
+
+F32 = mybir.dt.float32
+BF16 = mybir.dt.bfloat16
+I32 = mybir.dt.int32
+U32 = mybir.dt.uint32
+U16 = mybir.dt.uint16
+U8 = mybir.dt.uint8
+FP8X4 = mybir.dt.float8_e4m3fn_x4
+FP4X4 = mybir.dt.float4_e2m1fn_x4
+ACT = mybir.ActivationFunctionType
+ALU = mybir.AluOpType
+
+P = 128
+PACK = 4
+K_PASS = P * PACK
+PASSES = K // K_PASS
+HALF = 512
+HALVES = S // HALF
+CHUNK = 128
+N_TILES = N // P
+
+
+def tile_list_posting_term_scores_kernel(
+    tc, tab_words, tab_scales, offs, gT, w1, w4_words, w4_scales, wd_words, wd_scales, out
+):
+    nc = tc.nc
+    with ExitStack() as ctx:
+        keep = ctx.enter_context(tc.tile_pool(name="keep", bufs=1))
+        ring = ctx.enter_context(tc.tile_pool(name="ring", bufs=3))
+        logs = ctx.enter_context(tc.tile_pool(name="logs", bufs=6))
+        h_psum = ctx.enter_context(tc.psum_pool(name="h_psum", bufs=4))
+        y_psum = ctx.enter_context(tc.psum_pool(name="y_psum", bufs=4))
+
+        offsets = keep.tile([P, S // 16], U16, name="offsets")
+        nc.sync.dma_start(offsets[:], offs)
+
+        warm = keep.tile([P, 1], F32, name="warm")
+        warm_out = keep.tile([P, 1], F32, name="warm_out")
+        nc.vector.memset(warm[:], 1.0)
+        nc.scalar.activation(warm_out[:], warm[:], ACT.Ln)
+
+        tab_plane = keep.tile([P, T], U8, name="tab_plane", align_bytes=64)
+        wd_plane = keep.tile([P, N], U8, name="wd_plane", align_bytes=64)
+        w4_plane = keep.tile([P, PASSES, N], U8, name="w4_plane", align_bytes=64)
+        for plane in (tab_plane, wd_plane, w4_plane):
+            nc.vector.memset(plane[:].bitcast(I32), 0)
+
+        def load_packed_plane(plane, scales):
+            for q in range(4):
+                nc.sync.dma_start(
+                    plane[32 * q : 32 * q + 8, :].bitcast(I32), scales[:, 4 * q : 4 * q + 4, :].bitcast(I32)
+                )
+
+        def load_w1(b, a):
+            raw = keep.tile([P, PACK, K_PASS], F32, name="w1_raw%d%d" % (b, a))
+            rows = w1[K_PASS * a : K_PASS * (a + 1), K_PASS * b : K_PASS * (b + 1)]
+            nc.sync.dma_start(raw[:], rows.rearrange("(p j) c -> p j c", j=PACK))
+            return raw
+
+        def load_tab(a):
+            words = keep.tile([P, T], U32, name="tab%d" % a)
+            nc.sync.dma_start(words[:].bitcast(I32), tab_words[a].rearrange("p t i -> p (t i)").bitcast(I32))
+            return words
+
+        w1_raw = {}
+        tab = []
+        for a in range(PASSES):
+            w1_raw[0, a] = load_w1(0, a)
+            if a == 0:
+                load_packed_plane(tab_plane, tab_scales)
+            tab.append(load_tab(a))
+        for a in range(PASSES):
+            w1_raw[1, a] = load_w1(1, a)
+        load_packed_plane(wd_plane, wd_scales)
+        wd = keep.tile([P, PASSES, N], U32, name="wd", align_bytes=64)
+        nc.sync.dma_start(wd[:].bitcast(I32), wd_words.rearrange("a p c i -> p a (c i)").bitcast(I32))
+        w4 = keep.tile([P, PASSES, 2 * N], U8, name="w4", align_bytes=64)
+        nc.sync.dma_start(w4[:].bitcast(I32), w4_words.rearrange("a p c -> p a c").bitcast(I32))
+        g = []
+        for n in range(N_TILES):
+            g_tile = keep.tile([P, T], F32, name="g%d" % n)
+            nc.sync.dma_start(g_tile[:], gT[P * n : P * (n + 1), :])
+            g.append(g_tile)
+            if n == 0:
+                for q in range(4):
+                    nc.sync.dma_start(
+                        w4_plane[32 * q : 32 * q + 4, :, :].bitcast(I32),
+                        w4_scales[:, 4 * q : 4 * q + 4, :].rearrange("a r c -> r a c").bitcast(I32),
+                    )
+
+        def picks(half):
+            return offsets[:, half * HALF // 16 : (half + 1) * HALF // 16]
+
+        def gather_scales(half):
+            picked = keep.tile([P, HALF], U8, name="v_plane%d" % half, align_bytes=64)
+            nc.vector.tensor_copy(picked[:], tab_plane[:].indirect(picks(half)))
+            return picked
+
+        def gather_words(a, half):
+            picked = keep.tile([P, HALF], U32, name="v%d%d" % (a, half), align_bytes=64)
+            nc.vector.tensor_copy(picked[:], tab[a][:].indirect(picks(half)))
+            return picked
+
+        def quantize(grouped, name):
+            codes = keep.tile([P, HALF], U32, name=name + "_codes", align_bytes=64)
+            plane = keep.tile([P, HALF], U8, name=name + "_plane", align_bytes=64)
+            nc.vector.quantize_mx(out=codes[:].bitcast(FP8X4), scales=plane[:], in_=grouped[:])
+            return codes, plane
+
+        def prepare_w1(b, a):
+            grouped = ring.tile([P, PACK * K_PASS], BF16, name="w1_grouped", align_bytes=64)
+            dst = grouped[:].rearrange("p (t m j) -> p m t j", t=PACK, j=PACK)
+            src = w1_raw[b, a][:].rearrange("p j (m t) -> p m t j", t=PACK)
+            if b == 0:
+                nc.scalar.copy(dst, src)
+            else:
+                nc.vector.tensor_copy(dst, src)
+            return quantize(grouped, "w1q%d%d" % (b, a))
+
+        v_plane = [gather_scales(half) for half in range(HALVES)]
+        v = {}
+        w1q = {}
+        for a in range(PASSES):
+            v[a, 0] = gather_words(a, 0)
+            w1q[0, a] = prepare_w1(0, a)
+            v[a, 1] = gather_words(a, 1)
+        for a in range(PASSES):
+            w1q[1, a] = prepare_w1(1, a)
+
+        def hidden(b, half):
+            grouped = ring.tile([P, PACK * HALF], BF16, name="h_grouped", align_bytes=64)
+            for c in range(HALF // CHUNK):
+                cols = slice(CHUNK * c, CHUNK * (c + 1))
+                bank = h_psum.tile([P, PACK, CHUNK], F32, name="h_bank")
+                for a in range(PASSES):
+                    for t in range(PACK):
+                        codes, plane = w1q[b, a]
+                        nc.tensor.matmul_mx(
+                            out=bank[:, t, :],
+                            lhsT=codes[:, P * t : P * (t + 1)].bitcast(FP8X4),
+                            lhsT_scale=plane[:, P * t : P * (t + 1)],
+                            rhs=v[a, half][:, cols].bitcast(FP8X4),
+                            rhs_scale=v_plane[half][4 * a :, cols],
+                            start=(a == 0 and t == 0),
+                            stop=(a == PASSES - 1 and t == PACK - 1),
+                        )
+                dst = grouped[:, PACK * CHUNK * c : PACK * CHUNK * (c + 1)].rearrange("p (n t) -> p n t", t=PACK)
+                src = bank[:].rearrange("p t n -> p n t")
+                if b == 1 and half == 0 and c % 2 == 1:
+                    nc.vector.tensor_scalar_max(dst, src, 0.0)
+                else:
+                    nc.scalar.activation(dst, src, ACT.Relu)
+            return quantize(grouped, "hq%d%d" % (b, half))
+
+        hq = {}
+        scores = [keep.tile([P, S], F32, name="scores%d" % n) for n in range(N_TILES)]
+
+        def score(n, half):
+            terms = slice(P * n, P * (n + 1))
+            docs = slice(HALF * half, HALF * (half + 1))
+            bank = y_psum.tile([P, HALF], F32, name="y_bank")
+            for a in range(PASSES):
+                nc.tensor.matmul_mx(
+                    out=bank[:],
+                    lhsT=wd[:, a, terms].bitcast(FP8X4),
+                    lhsT_scale=wd_plane[4 * a :, terms],
+                    rhs=v[a, half][:].bitcast(FP8X4),
+                    rhs_scale=v_plane[half][4 * a :, :],
+                    start=(a == 0),
+                    stop=False,
+                )
+            for b in range(PASSES):
+                codes, plane = hq[b, half]
+                nc.tensor.matmul_mx(
+                    out=bank[:],
+                    lhsT=w4[:, b, 2 * P * n : 2 * P * (n + 1)].bitcast(FP4X4),
+                    lhsT_scale=w4_plane[:, b, terms],
+                    rhs=codes[:].bitcast(FP8X4),
+                    rhs_scale=plane[:],
+                    start=False,
+                    stop=(b == PASSES - 1),
+                )
+            cut = ring.tile([P, HALF], F32, name="cut")
+            nc.scalar.activation(cut[:], bank[:], ACT.Relu)
+            log = logs.tile([P, HALF], F32, name="log")
+            nc.scalar.activation(log[:], cut[:], ACT.Ln, bias=1.0)
+            nc.vector.tensor_tensor(scores[n][:, docs], g[n][:].indirect(picks(half)), log[:], ALU.mult)
+            if n == N_TILES - 1:
+                nc.sync.dma_start(out[terms, docs], scores[n][:, docs])
+            elif half == HALVES - 1:
+                nc.sync.dma_start(out[terms, :], scores[n][:])
+
+        hq[0, 0] = hidden(0, 0)
+        hq[0, 1] = hidden(0, 1)
+        hq[1, 0] = hidden(1, 0)
+        score(0, 0)
+        hq[1, 1] = hidden(1, 1)
+        score(1, 0)
+        score(0, 1)
+        score(1, 1)
+        for n in range(2, N_TILES):
+            for half in range(HALVES):
+                score(n, half)

@@ -33,12 +33,10 @@ def tile_list_posting_term_scores_kernel(
     with ExitStack() as ctx:
         keep = ctx.enter_context(tc.tile_pool(name="keep", bufs=1))
         ring = ctx.enter_context(tc.tile_pool(name="ring", bufs=3))
-        logs = ctx.enter_context(tc.tile_pool(name="logs", bufs=6))
-        h_psum = ctx.enter_context(tc.psum_pool(name="h_psum", bufs=4))
-        y_psum = ctx.enter_context(tc.psum_pool(name="y_psum", bufs=4))
+        logs = ctx.enter_context(tc.tile_pool(name="logs", bufs=4))
+        psum = ctx.enter_context(tc.psum_pool(name="psum", bufs=1))
 
         offsets = keep.tile([P, S // 16], U16, name="offsets")
-        nc.sync.dma_start(offsets[:], offs)
 
         warm = keep.tile([P, 1], F32, name="warm")
         warm_out = keep.tile([P, 1], F32, name="warm_out")
@@ -73,11 +71,19 @@ def tile_list_posting_term_scores_kernel(
         for a in range(PASSES):
             w1_raw[0, a] = load_w1(0, a)
             if a == 0:
+                nc.sync.dma_start(offsets[:], offs)
                 load_packed_plane(tab_plane, tab_scales)
+            else:
+                load_packed_plane(wd_plane, wd_scales)
             tab.append(load_tab(a))
         for a in range(PASSES):
             w1_raw[1, a] = load_w1(1, a)
-        load_packed_plane(wd_plane, wd_scales)
+            if a == 0:
+                for q in range(4):
+                    nc.sync.dma_start(
+                        w4_plane[32 * q : 32 * q + 4, :, :].bitcast(I32),
+                        w4_scales[:, 4 * q : 4 * q + 4, :].rearrange("a r c -> r a c").bitcast(I32),
+                    )
         wd = keep.tile([P, PASSES, N], U32, name="wd", align_bytes=64)
         nc.sync.dma_start(wd[:].bitcast(I32), wd_words.rearrange("a p c i -> p a (c i)").bitcast(I32))
         w4 = keep.tile([P, PASSES, 2 * N], U8, name="w4", align_bytes=64)
@@ -87,12 +93,6 @@ def tile_list_posting_term_scores_kernel(
             g_tile = keep.tile([P, T], F32, name="g%d" % n)
             nc.sync.dma_start(g_tile[:], gT[P * n : P * (n + 1), :])
             g.append(g_tile)
-            if n == 0:
-                for q in range(4):
-                    nc.sync.dma_start(
-                        w4_plane[32 * q : 32 * q + 4, :, :].bitcast(I32),
-                        w4_scales[:, 4 * q : 4 * q + 4, :].rearrange("a r c -> r a c").bitcast(I32),
-                    )
 
         def picks(half):
             return offsets[:, half * HALF // 16 : (half + 1) * HALF // 16]
@@ -107,14 +107,14 @@ def tile_list_posting_term_scores_kernel(
             nc.vector.tensor_copy(picked[:], tab[a][:].indirect(picks(half)))
             return picked
 
-        def quantize(grouped, name):
-            codes = keep.tile([P, HALF], U32, name=name + "_codes", align_bytes=64)
+        def quantize(grouped, name, tag=None):
+            codes = keep.tile([P, HALF], U32, name=name + "_codes", tag=tag or name, align_bytes=64)
             plane = keep.tile([P, HALF], U8, name=name + "_plane", align_bytes=64)
             nc.vector.quantize_mx(out=codes[:].bitcast(FP8X4), scales=plane[:], in_=grouped[:])
             return codes, plane
 
         def prepare_w1(b, a):
-            grouped = ring.tile([P, PACK * K_PASS], BF16, name="w1_grouped", align_bytes=64)
+            grouped = keep.tile([P, PACK * K_PASS], BF16, name="w1_grouped%d%d" % (b, a), align_bytes=64)
             dst = grouped[:].rearrange("p (t m j) -> p m t j", t=PACK, j=PACK)
             src = w1_raw[b, a][:].rearrange("p j (m t) -> p m t j", t=PACK)
             if b == 0:
@@ -134,10 +134,11 @@ def tile_list_posting_term_scores_kernel(
             w1q[1, a] = prepare_w1(1, a)
 
         def hidden(b, half):
-            grouped = ring.tile([P, PACK * HALF], BF16, name="h_grouped", align_bytes=64)
+            grouped = keep.tile([P, PACK * HALF], BF16, name="h_grouped%d%d" % (b, half), align_bytes=64)
             for c in range(HALF // CHUNK):
                 cols = slice(CHUNK * c, CHUNK * (c + 1))
-                bank = h_psum.tile([P, PACK, CHUNK], F32, name="h_bank")
+                first = 4 if (b, half) == (0, 1) else 0
+                bank = psum.tile([P, PACK, CHUNK], F32, name="h_bank", tag="bank%d" % (first + c))
                 for a in range(PASSES):
                     for t in range(PACK):
                         codes, plane = w1q[b, a]
@@ -152,19 +153,20 @@ def tile_list_posting_term_scores_kernel(
                         )
                 dst = grouped[:, PACK * CHUNK * c : PACK * CHUNK * (c + 1)].rearrange("p (n t) -> p n t", t=PACK)
                 src = bank[:].rearrange("p t n -> p n t")
-                if b == 1 and half == 0 and c % 2 == 1:
+                if (b, half, c) in ((1, 0, 0), (1, 0, 2)):
                     nc.vector.tensor_scalar_max(dst, src, 0.0)
                 else:
                     nc.scalar.activation(dst, src, ACT.Relu)
-            return quantize(grouped, "hq%d%d" % (b, half))
+            return grouped
 
         hq = {}
+        units = [(n, half) for half in range(HALVES) for n in range(3)]
+        units = units + [(n, half) for n in range(3, N_TILES) for half in range(HALVES)]
         scores = [keep.tile([P, S], F32, name="scores%d" % n) for n in range(N_TILES)]
 
-        def score(n, half):
+        def logits(n, half):
             terms = slice(P * n, P * (n + 1))
-            docs = slice(HALF * half, HALF * (half + 1))
-            bank = y_psum.tile([P, HALF], F32, name="y_bank")
+            bank = psum.tile([P, HALF], F32, name="y_bank", tag="bank%d" % ((4 + units.index((n, half))) % 8))
             for a in range(PASSES):
                 nc.tensor.matmul_mx(
                     out=bank[:],
@@ -188,22 +190,30 @@ def tile_list_posting_term_scores_kernel(
                 )
             cut = ring.tile([P, HALF], F32, name="cut")
             nc.scalar.activation(cut[:], bank[:], ACT.Relu)
+            return cut
+
+        def score(n, half, cut):
+            terms = slice(P * n, P * (n + 1))
+            docs = slice(HALF * half, HALF * (half + 1))
             log = logs.tile([P, HALF], F32, name="log")
             nc.scalar.activation(log[:], cut[:], ACT.Ln, bias=1.0)
-            nc.vector.tensor_tensor(scores[n][:, docs], g[n][:].indirect(picks(half)), log[:], ALU.mult)
+            weights = g0_picked[:, docs] if n == 0 else g[n][:].indirect(picks(half))
+            nc.vector.tensor_tensor(scores[n][:, docs], weights, log[:], ALU.mult)
             if n == N_TILES - 1:
                 nc.sync.dma_start(out[terms, docs], scores[n][:, docs])
             elif half == HALVES - 1:
                 nc.sync.dma_start(out[terms, :], scores[n][:])
 
-        hq[0, 0] = hidden(0, 0)
-        hq[0, 1] = hidden(0, 1)
-        hq[1, 0] = hidden(1, 0)
-        score(0, 0)
-        hq[1, 1] = hidden(1, 1)
-        score(1, 0)
-        score(0, 1)
-        score(1, 1)
-        for n in range(2, N_TILES):
-            for half in range(HALVES):
-                score(n, half)
+        hq[0, 0] = quantize(hidden(0, 0), "hq00", "w1_grouped11")
+        late = hidden(0, 1)
+        hq[1, 0] = quantize(hidden(1, 0), "hq10")
+        hq[0, 1] = quantize(late, "hq01", "h_grouped10")
+        g0_picked = keep.tile([P, S], F32, name="g0_picked", tag="h_grouped01", align_bytes=64)
+        nc.vector.tensor_copy(g0_picked[:], g[0][:].indirect(offsets[:]))
+        score(0, 0, logits(0, 0))
+        cut = logits(1, 0)
+        hq[1, 1] = quantize(hidden(1, 1), "hq11")
+        for now, ahead in zip(units[1:], units[2:] + [None]):
+            cut_ahead = logits(*ahead) if ahead else None
+            score(now[0], now[1], cut)
+            cut = cut_ahead

from contextlib import ExitStack

import concourse.mybir as mybir

T, S, K, H, N = 2048, 1024, 1024, 1024, 768
FLOPS = 2 * S * (K * H + H * N + K * N)

F32 = mybir.dt.float32
BF16 = mybir.dt.bfloat16
I32 = mybir.dt.int32
U32 = mybir.dt.uint32
U16 = mybir.dt.uint16
U8 = mybir.dt.uint8
FP8X4 = mybir.dt.float8_e4m3fn_x4
FP4X4 = mybir.dt.float4_e2m1fn_x4
ACT = mybir.ActivationFunctionType
ALU = mybir.AluOpType

P = 128
PACK = 4
K_PASS = P * PACK
PASSES = K // K_PASS
HALF = 512
HALVES = S // HALF
CHUNK = 128
N_TILES = N // P


def tile_list_posting_term_scores_kernel(
    tc, tab_words, tab_scales, offs, gT, w1, w4_words, w4_scales, wd_words, wd_scales, out
):
    nc = tc.nc
    with ExitStack() as ctx:
        keep = ctx.enter_context(tc.tile_pool(name="keep", bufs=1))
        ring = ctx.enter_context(tc.tile_pool(name="ring", bufs=3))
        logs = ctx.enter_context(tc.tile_pool(name="logs", bufs=4))
        psum = ctx.enter_context(tc.psum_pool(name="psum", bufs=1))

        offsets = keep.tile([P, S // 16], U16, name="offsets")

        warm = keep.tile([P, 1], F32, name="warm")
        warm_out = keep.tile([P, 1], F32, name="warm_out")
        nc.vector.memset(warm[:], 1.0)
        nc.scalar.activation(warm_out[:], warm[:], ACT.Ln)

        tab_plane = keep.tile([P, T], U8, name="tab_plane", align_bytes=64)
        wd_plane = keep.tile([P, N], U8, name="wd_plane", align_bytes=64)
        w4_plane = keep.tile([P, PASSES, N], U8, name="w4_plane", align_bytes=64)
        for plane in (tab_plane, wd_plane, w4_plane):
            nc.vector.memset(plane[:].bitcast(I32), 0)

        def load_packed_plane(plane, scales):
            for q in range(4):
                nc.sync.dma_start(
                    plane[32 * q : 32 * q + 8, :].bitcast(I32), scales[:, 4 * q : 4 * q + 4, :].bitcast(I32)
                )

        def load_w1(b, a):
            raw = keep.tile([P, PACK, K_PASS], F32, name="w1_raw%d%d" % (b, a))
            rows = w1[K_PASS * a : K_PASS * (a + 1), K_PASS * b : K_PASS * (b + 1)]
            nc.sync.dma_start(raw[:], rows.rearrange("(p j) c -> p j c", j=PACK))
            return raw

        def load_tab(a):
            words = keep.tile([P, T], U32, name="tab%d" % a)
            nc.sync.dma_start(words[:].bitcast(I32), tab_words[a].rearrange("p t i -> p (t i)").bitcast(I32))
            return words

        w1_raw = {}
        tab = []
        for a in range(PASSES):
            w1_raw[0, a] = load_w1(0, a)
            if a == 0:
                nc.sync.dma_start(offsets[:], offs)
                load_packed_plane(tab_plane, tab_scales)
            else:
                load_packed_plane(wd_plane, wd_scales)
            tab.append(load_tab(a))
        for a in range(PASSES):
            w1_raw[1, a] = load_w1(1, a)
            if a == 0:
                for q in range(4):
                    nc.sync.dma_start(
                        w4_plane[32 * q : 32 * q + 4, :, :].bitcast(I32),
                        w4_scales[:, 4 * q : 4 * q + 4, :].rearrange("a r c -> r a c").bitcast(I32),
                    )
        wd = keep.tile([P, PASSES, N], U32, name="wd", align_bytes=64)
        nc.sync.dma_start(wd[:].bitcast(I32), wd_words.rearrange("a p c i -> p a (c i)").bitcast(I32))
        w4 = keep.tile([P, PASSES, 2 * N], U8, name="w4", align_bytes=64)
        nc.sync.dma_start(w4[:].bitcast(I32), w4_words.rearrange("a p c -> p a c").bitcast(I32))
        g = []
        for n in range(N_TILES):
            g_tile = keep.tile([P, T], F32, name="g%d" % n)
            nc.sync.dma_start(g_tile[:], gT[P * n : P * (n + 1), :])
            g.append(g_tile)

        def picks(half):
            return offsets[:, half * HALF // 16 : (half + 1) * HALF // 16]

        def gather_scales(half):
            picked = keep.tile([P, HALF], U8, name="v_plane%d" % half, align_bytes=64)
            nc.vector.tensor_copy(picked[:], tab_plane[:].indirect(picks(half)))
            return picked

        def gather_words(a, half):
            picked = keep.tile([P, HALF], U32, name="v%d%d" % (a, half), align_bytes=64)
            nc.vector.tensor_copy(picked[:], tab[a][:].indirect(picks(half)))
            return picked

        def quantize(grouped, name, tag=None):
            codes = keep.tile([P, HALF], U32, name=name + "_codes", tag=tag or name, align_bytes=64)
            plane = keep.tile([P, HALF], U8, name=name + "_plane", align_bytes=64)
            nc.vector.quantize_mx(out=codes[:].bitcast(FP8X4), scales=plane[:], in_=grouped[:])
            return codes, plane

        def prepare_w1(b, a):
            grouped = keep.tile([P, PACK * K_PASS], BF16, name="w1_grouped%d%d" % (b, a), align_bytes=64)
            dst = grouped[:].rearrange("p (t m j) -> p m t j", t=PACK, j=PACK)
            src = w1_raw[b, a][:].rearrange("p j (m t) -> p m t j", t=PACK)
            if b == 0:
                nc.scalar.copy(dst, src)
            else:
                nc.vector.tensor_copy(dst, src)
            return quantize(grouped, "w1q%d%d" % (b, a))

        v_plane = [gather_scales(half) for half in range(HALVES)]
        v = {}
        w1q = {}
        for a in range(PASSES):
            v[a, 0] = gather_words(a, 0)
            w1q[0, a] = prepare_w1(0, a)
            v[a, 1] = gather_words(a, 1)
        for a in range(PASSES):
            w1q[1, a] = prepare_w1(1, a)

        def hidden(b, half):
            grouped = keep.tile([P, PACK * HALF], BF16, name="h_grouped%d%d" % (b, half), align_bytes=64)
            for c in range(HALF // CHUNK):
                cols = slice(CHUNK * c, CHUNK * (c + 1))
                first = 4 if (b, half) == (0, 1) else 0
                bank = psum.tile([P, PACK, CHUNK], F32, name="h_bank", tag="bank%d" % (first + c))
                for a in range(PASSES):
                    for t in range(PACK):
                        codes, plane = w1q[b, a]
                        nc.tensor.matmul_mx(
                            out=bank[:, t, :],
                            lhsT=codes[:, P * t : P * (t + 1)].bitcast(FP8X4),
                            lhsT_scale=plane[:, P * t : P * (t + 1)],
                            rhs=v[a, half][:, cols].bitcast(FP8X4),
                            rhs_scale=v_plane[half][4 * a :, cols],
                            start=(a == 0 and t == 0),
                            stop=(a == PASSES - 1 and t == PACK - 1),
                        )
                dst = grouped[:, PACK * CHUNK * c : PACK * CHUNK * (c + 1)].rearrange("p (n t) -> p n t", t=PACK)
                src = bank[:].rearrange("p t n -> p n t")
                if (b, half, c) in ((1, 0, 0), (1, 0, 2)):
                    nc.vector.tensor_scalar_max(dst, src, 0.0)
                else:
                    nc.scalar.activation(dst, src, ACT.Relu)
            return grouped

        hq = {}
        units = [(n, half) for half in range(HALVES) for n in range(3)]
        units = units + [(n, half) for n in range(3, N_TILES) for half in range(HALVES)]
        scores = [keep.tile([P, S], F32, name="scores%d" % n) for n in range(N_TILES)]

        def logits(n, half):
            terms = slice(P * n, P * (n + 1))
            bank = psum.tile([P, HALF], F32, name="y_bank", tag="bank%d" % ((4 + units.index((n, half))) % 8))
            for a in range(PASSES):
                nc.tensor.matmul_mx(
                    out=bank[:],
                    lhsT=wd[:, a, terms].bitcast(FP8X4),
                    lhsT_scale=wd_plane[4 * a :, terms],
                    rhs=v[a, half][:].bitcast(FP8X4),
                    rhs_scale=v_plane[half][4 * a :, :],
                    start=(a == 0),
                    stop=False,
                )
            for b in range(PASSES):
                codes, plane = hq[b, half]
                nc.tensor.matmul_mx(
                    out=bank[:],
                    lhsT=w4[:, b, 2 * P * n : 2 * P * (n + 1)].bitcast(FP4X4),
                    lhsT_scale=w4_plane[:, b, terms],
                    rhs=codes[:].bitcast(FP8X4),
                    rhs_scale=plane[:],
                    start=False,
                    stop=(b == PASSES - 1),
                )
            cut = ring.tile([P, HALF], F32, name="cut")
            nc.scalar.activation(cut[:], bank[:], ACT.Relu)
            return cut

        def score(n, half, cut):
            terms = slice(P * n, P * (n + 1))
            docs = slice(HALF * half, HALF * (half + 1))
            log = logs.tile([P, HALF], F32, name="log")
            nc.scalar.activation(log[:], cut[:], ACT.Ln, bias=1.0)
            weights = g0_picked[:, docs] if n == 0 else g[n][:].indirect(picks(half))
            nc.vector.tensor_tensor(scores[n][:, docs], weights, log[:], ALU.mult)
            if n == N_TILES - 1:
                nc.sync.dma_start(out[terms, docs], scores[n][:, docs])
            elif half == HALVES - 1:
                nc.sync.dma_start(out[terms, :], scores[n][:])

        hq[0, 0] = quantize(hidden(0, 0), "hq00", "w1_grouped11")
        late = hidden(0, 1)
        hq[1, 0] = quantize(hidden(1, 0), "hq10")
        hq[0, 1] = quantize(late, "hq01", "h_grouped10")
        g0_picked = keep.tile([P, S], F32, name="g0_picked", tag="h_grouped01", align_bytes=64)
        nc.vector.tensor_copy(g0_picked[:], g[0][:].indirect(offsets[:]))
        score(0, 0, logits(0, 0))
        cut = logits(1, 0)
        hq[1, 1] = quantize(hidden(1, 1), "hq11")
        for now, ahead in zip(units[1:], units[2:] + [None]):
            cut_ahead = logits(*ahead) if ahead else None
            score(now[0], now[1], cut)
            cut = cut_ahead
